import numpy as np
import ml_dtypes


def mxq(x, axis, fmt="e4m3"):
    dtype, down = {"e4m3": (ml_dtypes.float8_e4m3fn, 7), "e5m2": (ml_dtypes.float8_e5m2, 14)}[fmt]
    v = np.moveaxis(np.asarray(x, np.float32).astype(ml_dtypes.bfloat16).astype(np.float64), axis, -1)
    blocks = v.reshape(v.shape[:-1] + (-1, 32))
    amax = np.abs(blocks).max(-1, keepdims=True)
    byte = np.maximum(np.where(amax > 0, np.frexp(amax)[1] - 1 + 127, 0) - down, 1)
    scale = np.exp2(byte - 127.0)
    codes = (blocks / scale).astype(np.float32).astype(dtype).astype(np.float64)
    return np.moveaxis((codes * scale).reshape(v.shape), -1, axis)


WIDE = False


def mx_kscale(k):
    if not WIDE:
        return np.ones(k)
    levels = np.array([30, -30])
    if k % 512:
        return np.exp2(np.random.permutation(np.resize(levels, k // 32))).repeat(32)
    a = np.empty((k // 512, 16))
    for p in range(k // 512):
        a[p, :8] = np.random.permutation(np.resize(levels, 8))
        for g in range(8):
            far = levels[np.abs(levels - a[p, g]) >= 10]
            a[p, g + 8] = far[np.random.randint(len(far))]
    return np.exp2(a.ravel()).repeat(32)


def f64(x):
    return np.asarray(x).astype(np.float64)


def striped(idx):
    return np.tile(np.asarray(idx).reshape(-1, 16).T, (8, 1)).astype(np.uint16)


def unstriped(offs):
    return offs[:16].T.reshape(-1).astype(np.int64)


E2M1 = np.array([0.0, 0.5, 1.0, 1.5, 2.0, 3.0, 4.0, 6.0, -0.0, -0.5, -1.0, -1.5, -2.0, -3.0, -4.0, -6.0])


def pack_weight(w, fmt):
    k, n = w.shape
    w = f64(np.asarray(w, np.float32).astype(ml_dtypes.bfloat16)).reshape(k // 32, 32, n)
    amax = np.abs(w).max(1)
    if fmt in ("e4m3", "e5m2"):
        byte = np.frexp(amax)[1] - 1 + 127 - (7 if fmt == "e4m3" else 14)
    else:
        mant, ex = np.frexp(amax / 6.0)
        byte = np.where(mant > 0.5, ex, ex - 1) + 127
    byte = np.clip(np.where(amax > 0, byte, 1), 1, 254)
    scaled = (w * np.exp2(127.0 - byte)[:, None, :]).reshape(k, n).astype(np.float32)
    by_word = np.ascontiguousarray(scaled.reshape(k // 512, 128, 4, n).transpose(0, 1, 3, 2))
    if fmt in ("e4m3", "e5m2"):
        words = by_word.astype(ml_dtypes.float8_e4m3fn if fmt == "e4m3" else ml_dtypes.float8_e5m2).view(np.uint8)
    else:
        c = by_word.astype(ml_dtypes.float4_e2m1fn).view(np.uint8) & 0xF
        words = (c[..., 0::2] | (c[..., 1::2] << 4)).reshape(k // 512, 128, 2 * n)
    return np.ascontiguousarray(words), np.ascontiguousarray(byte.astype(np.uint8).reshape(k // 512, 16, n))


def unpack_weight(words, scales, fmt):
    g, _, n = scales.shape
    words = np.ascontiguousarray(words).reshape(g, 128, n, -1)
    if fmt in ("e4m3", "e5m2"):
        vals = words.view(ml_dtypes.float8_e4m3fn if fmt == "e4m3" else ml_dtypes.float8_e5m2).astype(np.float64)
    else:
        nib = np.empty((g, 128, n, 4), np.uint8)
        nib[..., 0::2] = words & 0xF
        nib[..., 1::2] = words >> 4
        vals = E2M1[nib]
    vals = vals * np.repeat(np.exp2(scales.astype(np.float64) - 127.0), 8, axis=1)[..., None]
    return vals.transpose(0, 1, 3, 2).reshape(g * 512, n)


K, T, J, R, N = 512, 2048, 256, 512, 256


def setup_inputs():
    n = np.random.standard_normal
    idx = np.random.permutation(T)[:J]
    idx2 = np.random.permutation(T)[:J]
    idx3 = np.random.permutation(J)[:J]
    idx4 = np.random.permutation(J)[:J]
    fk = mx_kscale(K)
    fr = mx_kscale(R)
    xtp = pack_weight(n((K, T)) / fk[:, None], "e2m1")
    wp = pack_weight(n((K, R)) * 1 / np.sqrt(K) * fk[:, None] * fr, "e5m2")
    w2p = pack_weight(n((K, R)) * 1 / np.sqrt(K) * fk[:, None] * fr, "e4m3")
    wbp = pack_weight(n((R, N)) * 1 / np.sqrt(R) / fr[:, None], "e4m3")
    wsp = pack_weight(n((K, N)) * 1 / np.sqrt(K) * fk[:, None], "e4m3")
    return {
        "xt_words": xtp[0],
        "xt_scales": xtp[1],
        "w_words": wp[0],
        "w_scales": wp[1],
        "w2_words": w2p[0],
        "w2_scales": w2p[1],
        "wb_words": wbp[0],
        "wb_scales": wbp[1],
        "ws_words": wsp[0],
        "ws_scales": wsp[1],
        "offs": striped(idx),
        "offs2": striped(idx2),
        "offs3": striped(idx3),
        "offs4": striped(idx4),
    }


def reference(xt_words, xt_scales, w_words, w_scales, w2_words, w2_scales, wb_words, wb_scales, ws_words, ws_scales, offs, offs2, offs3, offs4):
    idx = unstriped(offs)
    idx2 = unstriped(offs2)
    idx3 = unstriped(offs3)
    idx4 = unstriped(offs4)
    xtu = unpack_weight(xt_words, xt_scales, "e2m1")
    wu = unpack_weight(w_words, w_scales, "e5m2")
    w2u = unpack_weight(w2_words, w2_scales, "e4m3")
    wbu = unpack_weight(wb_words, wb_scales, "e4m3")
    wsu = unpack_weight(ws_words, ws_scales, "e4m3")
    xtidxg = xtu[:, idx]
    a = wu.T @ xtidxg
    xtidx2g = xtu[:, idx2]
    b = w2u.T @ xtidx2g
    hid = np.maximum(a - b[:, idx3], b - a[:, idx4])
    hidq = mxq(hid, 0, "e5m2")
    y = wbu.T @ hidq + wsu.T @ xtidxg
    return y

@@ -1,0 +1,168 @@
+from contextlib import ExitStack
+
+import concourse.mybir as mybir
+
+F32 = mybir.dt.float32
+BF16 = mybir.dt.bfloat16
+I32 = mybir.dt.int32
+U32 = mybir.dt.uint32
+U16 = mybir.dt.uint16
+U8 = mybir.dt.uint8
+E4M3 = mybir.dt.float8_e4m3fn_x4
+E5M2 = mybir.dt.float8_e5m2_x4
+E2M1 = mybir.dt.float4_e2m1fn_x4
+COPY = mybir.ActivationFunctionType.Copy
+SUB = mybir.AluOpType.subtract
+MAX = mybir.AluOpType.max
+
+P = 128
+PACK = 4
+K, T, J, R, N = 512, 2048, 256, 512, 256
+HALF = J // 2
+FLOPS = 2 * J * (2 * K * R + R * N + K * N)
+
+
+def words_of(dram):
+    return dram[0].rearrange("p c t -> p (c t)").bitcast(I32)
+
+
+def load_scales_by_quadrant(queue, tile, dram, first=0):
+    for q in range(4):
+        queue.dma_start(out=tile[32 * q : 32 * q + 4, first : first + dram.shape[2]].bitcast(I32), in_=dram[0, 4 * q : 4 * q + 4, :].bitcast(I32))
+
+
+def tile_list_mutual_ahead_skip_plain_kernel(
+    tc, xt_words, xt_scales, w_words, w_scales, w2_words, w2_scales, wb_words, wb_scales, ws_words, ws_scales,
+    offs, offs2, offs3, offs4, out,
+):
+    nc = tc.nc
+    with ExitStack() as ctx:
+        sb = ctx.enter_context(tc.tile_pool(name="sb", bufs=1))
+        ps = ctx.enter_context(tc.psum_pool(name="ps", bufs=1))
+
+        def tile(name, width, dtype):
+            return sb.tile([P, width], dtype, name=name, align_bytes=64)
+
+        idx1, idx2, idx3, idx4 = (tile(f"idx{i}", J // 16, U16) for i in range(1, 5))
+        xw, xs = tile("xw", T, U16), tile("xs", T, U8)
+        w_raw, w2_raw = tile("w_raw", R, U32), tile("w2_raw", R, U32)
+        wsc_raw, w2sc_raw = tile("wsc_raw", R, U8), tile("w2sc_raw", R, U8)
+        w_del, w2_del = tile("w_del", R, U32), tile("w2_del", R, U32)
+        wsc_del, w2sc_del = tile("wsc_del", R, U8), tile("w2sc_del", R, U8)
+        x1w, x2w = tile("x1w", J, U16), tile("x2w", J, U16)
+        x1s, x2s = tile("x1s", J, U8), tile("x2s", J, U8)
+        a_sb, b_sb = tile("a_sb", (PACK + 1) * J, F32), tile("b_sb", PACK * J, F32)
+
+        nc.vector.memset(xs[:].bitcast(I32), 0)
+        nc.vector.memset(wsc_raw[:].bitcast(I32), 0)
+        nc.vector.memset(w2sc_raw[:].bitcast(I32), 0)
+        nc.vector.memset(a_sb[:, PACK * J :], 0.0)
+        nc.gpsimd.dma_start(out=xw[:].bitcast(I32), in_=xt_words[0].bitcast(I32))
+        nc.gpsimd.dma_start(out=w_raw[:].bitcast(I32), in_=words_of(w_words))
+        nc.gpsimd.dma_start(out=w2_raw[:].bitcast(I32), in_=words_of(w2_words))
+        nc.sync.dma_start(idx1[:], offs)
+        nc.sync.dma_start(idx2[:], offs2)
+        nc.sync.dma_start(idx4[:], offs4)
+        nc.sync.dma_start(idx3[:], offs3)
+        load_scales_by_quadrant(nc.sync, xs, xt_scales)
+        load_scales_by_quadrant(nc.sync, wsc_raw, w_scales)
+        load_scales_by_quadrant(nc.sync, w2sc_raw, w2_scales)
+
+        def deal_words(dst, src):
+            nc.scalar.copy(out=dst[:].rearrange("p (t m) -> p m t", t=PACK), in_=src[:].rearrange("p (m t) -> p m t", t=PACK))
+
+        def deal_scales(dst, src):
+            nc.vector.tensor_copy(out=dst[:].rearrange("p (t m) -> p t m", t=PACK), in_=src[:].rearrange("p (m t) -> p t m", t=PACK))
+
+        def plane(sbuf, t):
+            return sbuf[:, t * J : (t + 1) * J]
+
+
+        nc.vector.tensor_copy(x1s[:], xs[:].indirect(idx1[:]))
+        nc.vector.tensor_copy(x2s[:], xs[:].indirect(idx2[:]))
+        nc.vector.tensor_copy(x1w[:], xw[:].indirect(idx1[:]))
+        deal_words(w_del, w_raw)
+        deal_scales(wsc_del, wsc_raw)
+        nc.vector.tensor_copy(x2w[:], xw[:].indirect(idx2[:]))
+        deal_words(w2_del, w2_raw)
+        deal_scales(w2sc_del, w2sc_raw)
+        nc.sync.dma_start(out=w_raw[:, :N].bitcast(I32), in_=words_of(ws_words))
+        load_scales_by_quadrant(nc.sync, wsc_raw, ws_scales)
+        nc.sync.dma_start(out=w_raw[:, N:].bitcast(I32), in_=words_of(wb_words))
+        load_scales_by_quadrant(nc.sync, wsc_raw, wb_scales, N)
+
+        a_banks = [ps.tile([P, 2 * J], F32, name="a01"), ps.tile([P, J], F32, name="a2"), ps.tile([P, J], F32, name="a3")]
+        b_banks = [ps.tile([P, 2 * J], F32, name="b01"), ps.tile([P, J], F32, name="b2"), ps.tile([P, J], F32, name="b3")]
+        y_banks = [ps.tile([P, 2, HALF], F32, name=f"y{h}") for h in range(2)]
+
+        def acc(banks, t):
+            return banks[t - 1][:] if t >= 2 else banks[0][:, t * J : (t + 1) * J]
+
+        def first_stage(banks, words, scales, fmt, xwords, xscales, t):
+            cols = slice(t * P, (t + 1) * P)
+            nc.tensor.matmul_mx(
+                out=acc(banks, t), lhsT=words[:, cols].bitcast(fmt), lhsT_scale=scales[:, cols],
+                rhs=xwords[:].bitcast(E2M1), rhs_scale=xscales[:], start=True, stop=True,
+            )
+
+        down = (3, 2, 1, 0)
+        for t in down:
+            first_stage(a_banks, w_del, wsc_del, E5M2, x1w, x1s, t)
+        for t in down:
+            first_stage(b_banks, w2_del, w2sc_del, E4M3, x2w, x2s, t)
+        for h in range(2):
+            slots = slice(h * HALF, (h + 1) * HALF)
+            for nh in range(2):
+                cols = slice(nh * P, (nh + 1) * P)
+                nc.tensor.matmul_mx(
+                    out=y_banks[h][:, nh, :], lhsT=w_raw[:, cols].bitcast(E4M3), lhsT_scale=wsc_raw[:, cols],
+                    rhs=x1w[:, slots].bitcast(E2M1), rhs_scale=x1s[:, slots], start=(nh == 0), stop=False,
+                )
+
+        ga, d2 = tile("ga", PACK * J, F32), tile("d2", PACK * J, F32)
+        gb = [sb.tile([P, PACK, HALF], F32, name=f"gb{h}", align_bytes=64) for h in range(2)]
+        d1 = [sb.tile([P, PACK, HALF], F32, name=f"d1{h}", align_bytes=64) for h in range(2)]
+
+        def half_of(src, h):
+            return src[:, : PACK * J].rearrange("p (t j) -> p t j", t=PACK)[:, :, h * HALF : (h + 1) * HALF]
+
+        nc.scalar.copy(out=plane(a_sb, 3), in_=a_banks[2][:])
+        nc.scalar.copy(out=plane(a_sb, 2), in_=a_banks[1][:])
+        nc.vector.tensor_copy(out=a_sb[:, : 2 * J], in_=a_banks[0][:])
+        nc.vector.tensor_copy(out=plane(b_sb, 3), in_=b_banks[2][:])
+        nc.vector.tensor_copy(out=plane(b_sb, 2), in_=b_banks[1][:])
+        nc.vector.tensor_copy(out=b_sb[:, : 2 * J], in_=b_banks[0][:])
+        for t in down:
+            nc.scalar.activation(plane(ga, t), a_sb[:, t * J : (t + 2) * J].indirect(idx4[:]), COPY)
+        for h in range(2):
+            for t in down:
+                looked_up = plane(b_sb, t).indirect(idx3[:, h * 8 : (h + 1) * 8])
+                if h == 0 and t >= 2:
+                    nc.vector.tensor_copy(gb[h][:, t, :], looked_up)
+                else:
+                    nc.scalar.activation(gb[h][:, t, :], looked_up, COPY)
+        nc.vector.tensor_tensor(d2[:, 2 * J :], b_sb[:, 2 * J :], ga[:, 2 * J :], SUB)
+        nc.vector.tensor_tensor(d2[:, : 2 * J], b_sb[:, : 2 * J], ga[:, : 2 * J], SUB)
+
+        for h in range(2):
+            nc.vector.tensor_tensor(d1[h][:], half_of(a_sb, h), gb[h][:], SUB)
+            hid = tile(f"hid{h}", PACK * HALF, BF16)
+            hq, hs = tile(f"hq{h}", HALF, U32), tile(f"hs{h}", HALF, U8)
+            nc.vector.tensor_tensor(
+                hid[:].rearrange("p (c i t) -> p c t i", i=4, t=PACK),
+                d1[h][:].rearrange("p t (c i) -> p c t i", i=4),
+                half_of(d2, h).rearrange("p t (c i) -> p c t i", i=4),
+                MAX,
+            )
+            nc.vector.quantize_mx(out=hq[:].bitcast(E5M2), scales=hs[:], in_=hid[:])
+            for nh in range(2):
+                cols = slice(N + nh * P, N + (nh + 1) * P)
+                nc.tensor.matmul_mx(
+                    out=y_banks[h][:, nh, :], lhsT=w_raw[:, cols].bitcast(E4M3), lhsT_scale=wsc_raw[:, cols],
+                    rhs=hq[:].bitcast(E5M2), rhs_scale=hs[:], start=False, stop=(nh == 1),
+                )
+            y = sb.tile([P, 2, HALF], F32, name=f"y_sb{h}", align_bytes=64)
+            nc.scalar.copy(out=y[:], in_=y_banks[h][:])
+            nc.sync.dma_start(
+                out=out.rearrange("(nh p) j -> p nh j", p=P)[:, :, h * HALF : (h + 1) * HALF], in_=y[:]
+            )

@@ -26,8 +26,8 @@ def words_of(dram):
     return dram[0].rearrange("p c t -> p (c t)").bitcast(I32)
 
 
-def load_scales_by_quadrant(queue, tile, dram, first=0):
-    for q in range(4):
+def load_scale_rows(queue, tile, dram, first=0, quadrants=(0, 1, 2, 3)):
+    for q in quadrants:
         queue.dma_start(out=tile[32 * q : 32 * q + 4, first : first + dram.shape[2]].bitcast(I32), in_=dram[0, 4 * q : 4 * q + 4, :].bitcast(I32))
 
 
@@ -53,20 +53,21 @@ def tile_list_mutual_ahead_skip_plain_kernel(
         x1s, x2s = tile("x1s", J, U8), tile("x2s", J, U8)
         a_sb, b_sb = tile("a_sb", (PACK + 1) * J, F32), tile("b_sb", PACK * J, F32)
 
+        nc.gpsimd.memset(wsc_raw[:].bitcast(I32), 0)
         nc.vector.memset(xs[:].bitcast(I32), 0)
-        nc.vector.memset(wsc_raw[:].bitcast(I32), 0)
         nc.vector.memset(w2sc_raw[:].bitcast(I32), 0)
         nc.vector.memset(a_sb[:, PACK * J :], 0.0)
-        nc.gpsimd.dma_start(out=xw[:].bitcast(I32), in_=xt_words[0].bitcast(I32))
+        nc.sync.dma_start(idx1[:], offs)
+        load_scale_rows(nc.sync, wsc_raw, w_scales, quadrants=(0,))
+        nc.sync.dma_start(out=xw[:].bitcast(I32), in_=xt_words[0].bitcast(I32))
         nc.gpsimd.dma_start(out=w_raw[:].bitcast(I32), in_=words_of(w_words))
         nc.gpsimd.dma_start(out=w2_raw[:].bitcast(I32), in_=words_of(w2_words))
-        nc.sync.dma_start(idx1[:], offs)
+        load_scale_rows(nc.scalar, xs, xt_scales)
+        load_scale_rows(nc.sync, wsc_raw, w_scales, quadrants=(1, 2, 3))
         nc.sync.dma_start(idx2[:], offs2)
+        load_scale_rows(nc.sync, w2sc_raw, w2_scales)
         nc.sync.dma_start(idx4[:], offs4)
         nc.sync.dma_start(idx3[:], offs3)
-        load_scales_by_quadrant(nc.sync, xs, xt_scales)
-        load_scales_by_quadrant(nc.sync, wsc_raw, w_scales)
-        load_scales_by_quadrant(nc.sync, w2sc_raw, w2_scales)
 
         def deal_words(dst, src):
             nc.scalar.copy(out=dst[:].rearrange("p (t m) -> p m t", t=PACK), in_=src[:].rearrange("p (m t) -> p m t", t=PACK))
@@ -79,24 +80,24 @@ def tile_list_mutual_ahead_skip_plain_kernel(
 
 
         nc.vector.tensor_copy(x1s[:], xs[:].indirect(idx1[:]))
-        nc.vector.tensor_copy(x2s[:], xs[:].indirect(idx2[:]))
         nc.vector.tensor_copy(x1w[:], xw[:].indirect(idx1[:]))
         deal_words(w_del, w_raw)
         deal_scales(wsc_del, wsc_raw)
+        nc.vector.tensor_copy(x2s[:], xs[:].indirect(idx2[:]))
         nc.vector.tensor_copy(x2w[:], xw[:].indirect(idx2[:]))
         deal_words(w2_del, w2_raw)
         deal_scales(w2sc_del, w2sc_raw)
         nc.sync.dma_start(out=w_raw[:, :N].bitcast(I32), in_=words_of(ws_words))
-        load_scales_by_quadrant(nc.sync, wsc_raw, ws_scales)
+        load_scale_rows(nc.sync, wsc_raw, ws_scales)
         nc.sync.dma_start(out=w_raw[:, N:].bitcast(I32), in_=words_of(wb_words))
-        load_scales_by_quadrant(nc.sync, wsc_raw, wb_scales, N)
+        load_scale_rows(nc.sync, wsc_raw, wb_scales, N)
 
-        a_banks = [ps.tile([P, 2 * J], F32, name="a01"), ps.tile([P, J], F32, name="a2"), ps.tile([P, J], F32, name="a3")]
-        b_banks = [ps.tile([P, 2 * J], F32, name="b01"), ps.tile([P, J], F32, name="b2"), ps.tile([P, J], F32, name="b3")]
-        y_banks = [ps.tile([P, 2, HALF], F32, name=f"y{h}") for h in range(2)]
+        a_banks = [ps.tile([P, 2 * J], F32, name=f"a_bank{u}") for u in range(2)]
+        b_banks = [ps.tile([P, 2 * J], F32, name=f"b_bank{u}") for u in range(2)]
+        y_banks = [[ps.tile([P, HALF], F32, name=f"y{h}{nh}") for nh in range(2)] for h in range(2)]
 
         def acc(banks, t):
-            return banks[t - 1][:] if t >= 2 else banks[0][:, t * J : (t + 1) * J]
+            return banks[t // 2][:, (t % 2) * J : (t % 2 + 1) * J]
 
         def first_stage(banks, words, scales, fmt, xwords, xscales, t):
             cols = slice(t * P, (t + 1) * P)
@@ -115,8 +116,8 @@ def tile_list_mutual_ahead_skip_plain_kernel(
             for nh in range(2):
                 cols = slice(nh * P, (nh + 1) * P)
                 nc.tensor.matmul_mx(
-                    out=y_banks[h][:, nh, :], lhsT=w_raw[:, cols].bitcast(E4M3), lhsT_scale=wsc_raw[:, cols],
-                    rhs=x1w[:, slots].bitcast(E2M1), rhs_scale=x1s[:, slots], start=(nh == 0), stop=False,
+                    out=y_banks[h][nh][:], lhsT=w_raw[:, cols].bitcast(E4M3), lhsT_scale=wsc_raw[:, cols],
+                    rhs=x1w[:, slots].bitcast(E2M1), rhs_scale=x1s[:, slots], start=True, stop=False,
                 )
 
         ga, d2 = tile("ga", PACK * J, F32), tile("d2", PACK * J, F32)
@@ -126,11 +127,9 @@ def tile_list_mutual_ahead_skip_plain_kernel(
         def half_of(src, h):
             return src[:, : PACK * J].rearrange("p (t j) -> p t j", t=PACK)[:, :, h * HALF : (h + 1) * HALF]
 
-        nc.scalar.copy(out=plane(a_sb, 3), in_=a_banks[2][:])
-        nc.scalar.copy(out=plane(a_sb, 2), in_=a_banks[1][:])
-        nc.vector.tensor_copy(out=a_sb[:, : 2 * J], in_=a_banks[0][:])
-        nc.vector.tensor_copy(out=plane(b_sb, 3), in_=b_banks[2][:])
-        nc.vector.tensor_copy(out=plane(b_sb, 2), in_=b_banks[1][:])
+        nc.scalar.copy(out=a_sb[:, 2 * J : 4 * J], in_=a_banks[1][:])
+        nc.scalar.copy(out=a_sb[:, : 2 * J], in_=a_banks[0][:])
+        nc.vector.tensor_copy(out=b_sb[:, 2 * J :], in_=b_banks[1][:])
         nc.vector.tensor_copy(out=b_sb[:, : 2 * J], in_=b_banks[0][:])
         for t in down:
             nc.scalar.activation(plane(ga, t), a_sb[:, t * J : (t + 2) * J].indirect(idx4[:]), COPY)
@@ -158,11 +157,18 @@ def tile_list_mutual_ahead_skip_plain_kernel(
             for nh in range(2):
                 cols = slice(N + nh * P, N + (nh + 1) * P)
                 nc.tensor.matmul_mx(
-                    out=y_banks[h][:, nh, :], lhsT=w_raw[:, cols].bitcast(E4M3), lhsT_scale=wsc_raw[:, cols],
-                    rhs=hq[:].bitcast(E5M2), rhs_scale=hs[:], start=False, stop=(nh == 1),
+                    out=y_banks[h][nh][:], lhsT=w_raw[:, cols].bitcast(E4M3), lhsT_scale=wsc_raw[:, cols],
+                    rhs=hq[:].bitcast(E5M2), rhs_scale=hs[:], start=False, stop=True,
                 )
-            y = sb.tile([P, 2, HALF], F32, name=f"y_sb{h}", align_bytes=64)
-            nc.scalar.copy(out=y[:], in_=y_banks[h][:])
-            nc.sync.dma_start(
-                out=out.rearrange("(nh p) j -> p nh j", p=P)[:, :, h * HALF : (h + 1) * HALF], in_=y[:]
-            )
+            slots = slice(h * HALF, (h + 1) * HALF)
+            if h == 0:
+                y = sb.tile([P, 2, HALF], F32, name="y_first", align_bytes=64)
+                for nh in range(2):
+                    nc.scalar.copy(out=y[:, nh, :], in_=y_banks[h][nh][:])
+                nc.sync.dma_start(out=out.rearrange("(nh p) j -> p nh j", p=P)[:, :, slots], in_=y[:])
+            else:
+                y0, y1 = tile("y_last0", HALF, F32), tile("y_last1", HALF, F32)
+                nc.vector.tensor_copy(out=y0[:], in_=y_banks[h][0][:])
+                nc.sync.dma_start(out=out[:P, slots], in_=y0[:])
+                nc.scalar.copy(out=y1[:], in_=y_banks[h][1][:])
+                nc.scalar.dma_start(out=out[P:, slots], in_=y1[:])

@@ -40,23 +40,23 @@ def tile_list_mutual_ahead_skip_plain_kernel(
         sb = ctx.enter_context(tc.tile_pool(name="sb", bufs=1))
         ps = ctx.enter_context(tc.psum_pool(name="ps", bufs=1))
 
-        def tile(name, width, dtype):
-            return sb.tile([P, width], dtype, name=name, align_bytes=64)
+        def tile(name, width, dtype, tag=None):
+            return sb.tile([P, width], dtype, name=name, tag=tag or name, align_bytes=64)
 
         idx1, idx2, idx3, idx4 = (tile(f"idx{i}", J // 16, U16) for i in range(1, 5))
         xw, xs = tile("xw", T, U16), tile("xs", T, U8)
         w_raw, w2_raw = tile("w_raw", R, U32), tile("w2_raw", R, U32)
-        wsc_raw, w2sc_raw = tile("wsc_raw", R, U8), tile("w2sc_raw", R, U8)
+        wsc_raw, w2sc_raw = tile("wsc_raw", R, U8), tile("w2sc_raw", R, U8, tag="shared")
         w_del, w2_del = tile("w_del", R, U32), tile("w2_del", R, U32)
         wsc_del, w2sc_del = tile("wsc_del", R, U8), tile("w2sc_del", R, U8)
         x1w, x2w = tile("x1w", J, U16), tile("x2w", J, U16)
         x1s, x2s = tile("x1s", J, U8), tile("x2s", J, U8)
-        a_sb, b_sb = tile("a_sb", (PACK + 1) * J, F32), tile("b_sb", PACK * J, F32)
+        a_hi, b_sb = tile("a_hi", 3 * J, F32), tile("b_sb", PACK * J, F32)
 
         nc.gpsimd.memset(wsc_raw[:].bitcast(I32), 0)
         nc.vector.memset(xs[:].bitcast(I32), 0)
         nc.vector.memset(w2sc_raw[:].bitcast(I32), 0)
-        nc.vector.memset(a_sb[:, PACK * J :], 0.0)
+        nc.vector.memset(a_hi[:, 2 * J :], 0.0)
         nc.sync.dma_start(idx1[:], offs)
         load_scale_rows(nc.sync, wsc_raw, w_scales, quadrants=(0,))
         nc.sync.dma_start(out=xw[:].bitcast(I32), in_=xt_words[0].bitcast(I32))
@@ -120,19 +120,23 @@ def tile_list_mutual_ahead_skip_plain_kernel(
                     rhs=x1w[:, slots].bitcast(E2M1), rhs_scale=x1s[:, slots], start=True, stop=False,
                 )
 
+        a_lo = tile("a_lo", 2 * J, F32, tag="shared")
         ga, d2 = tile("ga", PACK * J, F32), tile("d2", PACK * J, F32)
         gb = [sb.tile([P, PACK, HALF], F32, name=f"gb{h}", align_bytes=64) for h in range(2)]
         d1 = [sb.tile([P, PACK, HALF], F32, name=f"d1{h}", align_bytes=64) for h in range(2)]
 
-        def half_of(src, h):
-            return src[:, : PACK * J].rearrange("p (t j) -> p t j", t=PACK)[:, :, h * HALF : (h + 1) * HALF]
+        def half_of(src, h, planes=PACK):
+            return src[:, : planes * J].rearrange("p (t j) -> p t j", t=planes)[:, :, h * HALF : (h + 1) * HALF]
 
-        nc.scalar.copy(out=a_sb[:, 2 * J : 4 * J], in_=a_banks[1][:])
-        nc.scalar.copy(out=a_sb[:, : 2 * J], in_=a_banks[0][:])
+        nc.scalar.copy(out=a_hi[:, : 2 * J], in_=a_banks[1][:])
+        nc.vector.tensor_copy(out=a_lo[:], in_=a_banks[0][:])
         nc.vector.tensor_copy(out=b_sb[:, 2 * J :], in_=b_banks[1][:])
         nc.vector.tensor_copy(out=b_sb[:, : 2 * J], in_=b_banks[0][:])
-        for t in down:
-            nc.scalar.activation(plane(ga, t), a_sb[:, t * J : (t + 2) * J].indirect(idx4[:]), COPY)
+        nc.scalar.activation(plane(ga, 3), a_hi[:, J:].indirect(idx4[:]), COPY)
+        nc.scalar.activation(plane(ga, 2), a_hi[:, : 2 * J].indirect(idx4[:]), COPY)
+        for h in range(2):
+            nc.scalar.activation(ga[:, J + h * HALF : J + (h + 1) * HALF], a_lo[:, J:].indirect(idx4[:, h * 8 : (h + 1) * 8]), COPY)
+        nc.scalar.activation(plane(ga, 0), a_lo[:].indirect(idx4[:]), COPY)
         for h in range(2):
             for t in down:
                 looked_up = plane(b_sb, t).indirect(idx3[:, h * 8 : (h + 1) * 8])
@@ -140,11 +144,12 @@ def tile_list_mutual_ahead_skip_plain_kernel(
                     nc.vector.tensor_copy(gb[h][:, t, :], looked_up)
                 else:
                     nc.scalar.activation(gb[h][:, t, :], looked_up, COPY)
-        nc.vector.tensor_tensor(d2[:, 2 * J :], b_sb[:, 2 * J :], ga[:, 2 * J :], SUB)
-        nc.vector.tensor_tensor(d2[:, : 2 * J], b_sb[:, : 2 * J], ga[:, : 2 * J], SUB)
+        nc.gpsimd.tensor_tensor(d2[:, 2 * J :], b_sb[:, 2 * J :], ga[:, 2 * J :], SUB)
+        nc.vector.tensor_tensor(d2[:, : 2 * J], b_banks[0][:], ga[:, : 2 * J], SUB)
 
         for h in range(2):
-            nc.vector.tensor_tensor(d1[h][:], half_of(a_sb, h), gb[h][:], SUB)
+            nc.vector.tensor_tensor(d1[h][:, 2:, :], half_of(a_banks[1], h, 2), gb[h][:, 2:, :], SUB)
+            nc.vector.tensor_tensor(d1[h][:, :2, :], half_of(a_banks[0], h, 2), gb[h][:, :2, :], SUB)
             hid = tile(f"hid{h}", PACK * HALF, BF16)
             hq, hs = tile(f"hq{h}", HALF, U32), tile(f"hs{h}", HALF, U8)
             nc.vector.tensor_tensor(

from contextlib import ExitStack

import concourse.mybir as mybir

F32 = mybir.dt.float32
BF16 = mybir.dt.bfloat16
I32 = mybir.dt.int32
U32 = mybir.dt.uint32
U16 = mybir.dt.uint16
U8 = mybir.dt.uint8
E4M3 = mybir.dt.float8_e4m3fn_x4
E5M2 = mybir.dt.float8_e5m2_x4
E2M1 = mybir.dt.float4_e2m1fn_x4
COPY = mybir.ActivationFunctionType.Copy
SUB = mybir.AluOpType.subtract
MAX = mybir.AluOpType.max

P = 128
PACK = 4
K, T, J, R, N = 512, 2048, 256, 512, 256
HALF = J // 2
FLOPS = 2 * J * (2 * K * R + R * N + K * N)


def words_of(dram):
    return dram[0].rearrange("p c t -> p (c t)").bitcast(I32)


def load_scale_rows(queue, tile, dram, first=0, quadrants=(0, 1, 2, 3)):
    for q in quadrants:
        queue.dma_start(out=tile[32 * q : 32 * q + 4, first : first + dram.shape[2]].bitcast(I32), in_=dram[0, 4 * q : 4 * q + 4, :].bitcast(I32))


def tile_list_mutual_ahead_skip_plain_kernel(
    tc, xt_words, xt_scales, w_words, w_scales, w2_words, w2_scales, wb_words, wb_scales, ws_words, ws_scales,
    offs, offs2, offs3, offs4, out,
):
    nc = tc.nc
    with ExitStack() as ctx:
        sb = ctx.enter_context(tc.tile_pool(name="sb", bufs=1))
        ps = ctx.enter_context(tc.psum_pool(name="ps", bufs=1))

        def tile(name, width, dtype, tag=None):
            return sb.tile([P, width], dtype, name=name, tag=tag or name, align_bytes=64)

        idx1, idx2, idx3, idx4 = (tile(f"idx{i}", J // 16, U16) for i in range(1, 5))
        xw, xs = tile("xw", T, U16), tile("xs", T, U8)
        w_raw, w2_raw = tile("w_raw", R, U32), tile("w2_raw", R, U32)
        wsc_raw, w2sc_raw = tile("wsc_raw", R, U8), tile("w2sc_raw", R, U8, tag="shared")
        w_del, w2_del = tile("w_del", R, U32), tile("w2_del", R, U32)
        wsc_del, w2sc_del = tile("wsc_del", R, U8), tile("w2sc_del", R, U8)
        x1w, x2w = tile("x1w", J, U16), tile("x2w", J, U16)
        x1s, x2s = tile("x1s", J, U8), tile("x2s", J, U8)
        a_hi, b_sb = tile("a_hi", 3 * J, F32), tile("b_sb", PACK * J, F32)

        nc.gpsimd.memset(wsc_raw[:].bitcast(I32), 0)
        nc.vector.memset(xs[:].bitcast(I32), 0)
        nc.vector.memset(w2sc_raw[:].bitcast(I32), 0)
        nc.vector.memset(a_hi[:, 2 * J :], 0.0)
        nc.sync.dma_start(idx1[:], offs)
        load_scale_rows(nc.sync, wsc_raw, w_scales, quadrants=(0,))
        nc.sync.dma_start(out=xw[:].bitcast(I32), in_=xt_words[0].bitcast(I32))
        nc.gpsimd.dma_start(out=w_raw[:].bitcast(I32), in_=words_of(w_words))
        nc.gpsimd.dma_start(out=w2_raw[:].bitcast(I32), in_=words_of(w2_words))
        load_scale_rows(nc.scalar, xs, xt_scales)
        load_scale_rows(nc.sync, wsc_raw, w_scales, quadrants=(1, 2, 3))
        nc.sync.dma_start(idx2[:], offs2)
        load_scale_rows(nc.sync, w2sc_raw, w2_scales)
        nc.sync.dma_start(idx4[:], offs4)
        nc.sync.dma_start(idx3[:], offs3)

        def deal_words(dst, src):
            nc.scalar.copy(out=dst[:].rearrange("p (t m) -> p m t", t=PACK), in_=src[:].rearrange("p (m t) -> p m t", t=PACK))

        def deal_scales(dst, src):
            nc.vector.tensor_copy(out=dst[:].rearrange("p (t m) -> p t m", t=PACK), in_=src[:].rearrange("p (m t) -> p t m", t=PACK))

        def plane(sbuf, t):
            return sbuf[:, t * J : (t + 1) * J]


        nc.vector.tensor_copy(x1s[:], xs[:].indirect(idx1[:]))
        nc.vector.tensor_copy(x1w[:], xw[:].indirect(idx1[:]))
        deal_words(w_del, w_raw)
        deal_scales(wsc_del, wsc_raw)
        nc.vector.tensor_copy(x2s[:], xs[:].indirect(idx2[:]))
        nc.vector.tensor_copy(x2w[:], xw[:].indirect(idx2[:]))
        deal_words(w2_del, w2_raw)
        deal_scales(w2sc_del, w2sc_raw)
        nc.sync.dma_start(out=w_raw[:, :N].bitcast(I32), in_=words_of(ws_words))
        load_scale_rows(nc.sync, wsc_raw, ws_scales)
        nc.sync.dma_start(out=w_raw[:, N:].bitcast(I32), in_=words_of(wb_words))
        load_scale_rows(nc.sync, wsc_raw, wb_scales, N)

        a_banks = [ps.tile([P, 2 * J], F32, name=f"a_bank{u}") for u in range(2)]
        b_banks = [ps.tile([P, 2 * J], F32, name=f"b_bank{u}") for u in range(2)]
        y_banks = [[ps.tile([P, HALF], F32, name=f"y{h}{nh}") for nh in range(2)] for h in range(2)]

        def acc(banks, t):
            return banks[t // 2][:, (t % 2) * J : (t % 2 + 1) * J]

        def first_stage(banks, words, scales, fmt, xwords, xscales, t):
            cols = slice(t * P, (t + 1) * P)
            nc.tensor.matmul_mx(
                out=acc(banks, t), lhsT=words[:, cols].bitcast(fmt), lhsT_scale=scales[:, cols],
                rhs=xwords[:].bitcast(E2M1), rhs_scale=xscales[:], start=True, stop=True,
            )

        down = (3, 2, 1, 0)
        for t in down:
            first_stage(a_banks, w_del, wsc_del, E5M2, x1w, x1s, t)
        for t in down:
            first_stage(b_banks, w2_del, w2sc_del, E4M3, x2w, x2s, t)
        for h in range(2):
            slots = slice(h * HALF, (h + 1) * HALF)
            for nh in range(2):
                cols = slice(nh * P, (nh + 1) * P)
                nc.tensor.matmul_mx(
                    out=y_banks[h][nh][:], lhsT=w_raw[:, cols].bitcast(E4M3), lhsT_scale=wsc_raw[:, cols],
                    rhs=x1w[:, slots].bitcast(E2M1), rhs_scale=x1s[:, slots], start=True, stop=False,
                )

        a_lo = tile("a_lo", 2 * J, F32, tag="shared")
        ga, d2 = tile("ga", PACK * J, F32), tile("d2", PACK * J, F32)
        gb = [sb.tile([P, PACK, HALF], F32, name=f"gb{h}", align_bytes=64) for h in range(2)]
        d1 = [sb.tile([P, PACK, HALF], F32, name=f"d1{h}", align_bytes=64) for h in range(2)]

        def half_of(src, h, planes=PACK):
            return src[:, : planes * J].rearrange("p (t j) -> p t j", t=planes)[:, :, h * HALF : (h + 1) * HALF]

        nc.scalar.copy(out=a_hi[:, : 2 * J], in_=a_banks[1][:])
        nc.vector.tensor_copy(out=a_lo[:], in_=a_banks[0][:])
        nc.vector.tensor_copy(out=b_sb[:, 2 * J :], in_=b_banks[1][:])
        nc.vector.tensor_copy(out=b_sb[:, : 2 * J], in_=b_banks[0][:])
        nc.scalar.activation(plane(ga, 3), a_hi[:, J:].indirect(idx4[:]), COPY)
        nc.scalar.activation(plane(ga, 2), a_hi[:, : 2 * J].indirect(idx4[:]), COPY)
        for h in range(2):
            nc.scalar.activation(ga[:, J + h * HALF : J + (h + 1) * HALF], a_lo[:, J:].indirect(idx4[:, h * 8 : (h + 1) * 8]), COPY)
        nc.scalar.activation(plane(ga, 0), a_lo[:].indirect(idx4[:]), COPY)
        for h in range(2):
            for t in down:
                looked_up = plane(b_sb, t).indirect(idx3[:, h * 8 : (h + 1) * 8])
                if h == 0 and t >= 2:
                    nc.vector.tensor_copy(gb[h][:, t, :], looked_up)
                else:
                    nc.scalar.activation(gb[h][:, t, :], looked_up, COPY)
        nc.gpsimd.tensor_tensor(d2[:, 2 * J :], b_sb[:, 2 * J :], ga[:, 2 * J :], SUB)
        nc.vector.tensor_tensor(d2[:, : 2 * J], b_banks[0][:], ga[:, : 2 * J], SUB)

        for h in range(2):
            nc.vector.tensor_tensor(d1[h][:, 2:, :], half_of(a_banks[1], h, 2), gb[h][:, 2:, :], SUB)
            nc.vector.tensor_tensor(d1[h][:, :2, :], half_of(a_banks[0], h, 2), gb[h][:, :2, :], SUB)
            hid = tile(f"hid{h}", PACK * HALF, BF16)
            hq, hs = tile(f"hq{h}", HALF, U32), tile(f"hs{h}", HALF, U8)
            nc.vector.tensor_tensor(
                hid[:].rearrange("p (c i t) -> p c t i", i=4, t=PACK),
                d1[h][:].rearrange("p t (c i) -> p c t i", i=4),
                half_of(d2, h).rearrange("p t (c i) -> p c t i", i=4),
                MAX,
            )
            nc.vector.quantize_mx(out=hq[:].bitcast(E5M2), scales=hs[:], in_=hid[:])
            for nh in range(2):
                cols = slice(N + nh * P, N + (nh + 1) * P)
                nc.tensor.matmul_mx(
                    out=y_banks[h][nh][:], lhsT=w_raw[:, cols].bitcast(E4M3), lhsT_scale=wsc_raw[:, cols],
                    rhs=hq[:].bitcast(E5M2), rhs_scale=hs[:], start=False, stop=True,
                )
            slots = slice(h * HALF, (h + 1) * HALF)
            if h == 0:
                y = sb.tile([P, 2, HALF], F32, name="y_first", align_bytes=64)
                for nh in range(2):
                    nc.scalar.copy(out=y[:, nh, :], in_=y_banks[h][nh][:])
                nc.sync.dma_start(out=out.rearrange("(nh p) j -> p nh j", p=P)[:, :, slots], in_=y[:])
            else:
                y0, y1 = tile("y_last0", HALF, F32), tile("y_last1", HALF, F32)
                nc.vector.tensor_copy(out=y0[:], in_=y_banks[h][0][:])
                nc.sync.dma_start(out=out[:P, slots], in_=y0[:])
                nc.scalar.copy(out=y1[:], in_=y_banks[h][1][:])
                nc.scalar.dma_start(out=out[P:, slots], in_=y1[:])
